import numpy as np
import ml_dtypes


def mxq(x, axis, fmt="e4m3"):
    dtype, down = {"e4m3": (ml_dtypes.float8_e4m3fn, 7), "e5m2": (ml_dtypes.float8_e5m2, 14)}[fmt]
    v = np.moveaxis(np.asarray(x, np.float32).astype(ml_dtypes.bfloat16).astype(np.float64), axis, -1)
    blocks = v.reshape(v.shape[:-1] + (-1, 32))
    amax = np.abs(blocks).max(-1, keepdims=True)
    byte = np.maximum(np.where(amax > 0, np.frexp(amax)[1] - 1 + 127, 0) - down, 1)
    scale = np.exp2(byte - 127.0)
    codes = (blocks / scale).astype(np.float32).astype(dtype).astype(np.float64)
    return np.moveaxis((codes * scale).reshape(v.shape), -1, axis)


WIDE = False


def mx_kscale(k):
    if not WIDE:
        return np.ones(k)
    levels = np.array([10, -10, 5, -5, 0])
    if k % 512:
        return np.exp2(np.random.permutation(np.resize(levels, k // 32))).repeat(32)
    a = np.empty((k // 512, 16))
    for p in range(k // 512):
        a[p, :8] = np.random.permutation(np.resize(levels, 8))
        for g in range(8):
            far = levels[np.abs(levels - a[p, g]) >= 10]
            a[p, g + 8] = far[np.random.randint(len(far))]
    return np.exp2(a.ravel()).repeat(32)


BF16 = ml_dtypes.bfloat16


def bf(x):
    return np.asarray(x, np.float32).astype(BF16)


def f64(x):
    return np.asarray(x).astype(np.float64)

def planes(Y):
    n, m = Y.shape
    b = f64(bf(Y)).reshape(n // 32, 32, m)
    amax = np.abs(b).max(1)
    byte = np.clip(np.where(amax > 0, np.frexp(amax)[1] - 1 + 127 - 7, 1), 1, 254)
    codes = (b * np.exp2(127.0 - byte)[:, None, :]).reshape(n, m).astype(np.float32).astype(ml_dtypes.float8_e4m3fn).view(np.uint8)
    words = codes.reshape(n // 512, 128, 4, m).transpose(0, 1, 3, 2)
    return np.ascontiguousarray(words), np.ascontiguousarray(byte.astype(np.uint8).reshape(n // 512, 16, m))


NA, NB, NO, NV = 2048, 1536, 512, 1536

def setup_inputs():
    s = mx_kscale(NB)
    t = mx_kscale(NA)
    fock = 2.0 * np.random.randn(NA, NB) * t[:, None] * s[None, :]
    c_occ = np.random.randn(NB, NO) / np.sqrt(NB) / s[:, None]
    spread = np.exp(0.8 * np.random.randn(NV))
    c_virt = np.random.randn(NA, NV) / np.sqrt(NA) * spread[None, :] / t[:, None]
    shift_block = np.random.randn(NA, NO) * t[:, None]
    shift = 1.0 + 0.3 * np.random.randn(NO)
    e_occ = -0.5 - 0.5 * np.abs(np.random.randn(NO))
    e_virt = 0.5 + np.abs(np.random.randn(NV))
    return {"fock": bf(fock), "c_occ": bf(c_occ), "shift_block": bf(shift_block), "shift": bf(shift),
            "c_virt": bf(c_virt), "e_occ": bf(e_occ), "e_virt": bf(e_virt)}

def reference(fock, c_occ, shift_block, shift, c_virt, e_occ, e_virt):
    half = mxq(f64(fock), 1, "e4m3") @ mxq(f64(c_occ), 0, "e4m3")
    r = half + f64(shift_block) * f64(shift)[None, :]
    g = mxq(f64(c_virt), 0, "e4m3").T @ mxq(r, 0, "e4m3")
    y = g / (f64(e_occ)[None, :] - f64(e_virt)[:, None])
    Y = y.reshape(NV, NO)
    words, scales = planes(Y)
    return y, words, scales

@@ -1,0 +1,384 @@
+from contextlib import ExitStack
+
+import concourse.mybir as mybir
+from concourse.masks import make_identity
+
+NA, NB, NO, NV = 2048, 1536, 512, 1536
+FLOPS = 2 * NA * NB * NO + 2 * NA * NV * NO
+
+F32 = mybir.dt.float32
+BF16 = mybir.dt.bfloat16
+I32 = mybir.dt.int32
+U32 = mybir.dt.uint32
+U8 = mybir.dt.uint8
+FP8X4 = mybir.dt.float8_e4m3fn_x4
+ACT = mybir.ActivationFunctionType
+ALU = mybir.AluOpType
+
+P = 128
+PACK = 4
+KP = P * PACK
+NU_PASSES = NB // KP
+MU_BLOCKS = NA // KP
+V_BLOCKS = NV // KP
+HALVES = 2 * MU_BLOCKS
+CV_UNITS = V_BLOCKS * MU_BLOCKS
+FRAC_A, FRAC_B, SPLIT = 5, 9, 288
+STEP_UNITS = [[0], [1], [], [2], [3], [], [4], [5]]
+
+
+def tile_shifted_fock_amplitudes_h3_kernel(
+    tc, fock, c_occ, shift_block, shift, c_virt, e_occ, e_virt, out_0, out_1, out_2
+):
+    nc = tc.nc
+    with ExitStack() as ctx:
+        keep = ctx.enter_context(tc.tile_pool(name="keep", bufs=1))
+        flow = ctx.enter_context(tc.tile_pool(name="flow", bufs=2))
+        psum = ctx.enter_context(tc.psum_pool(name="psum", bufs=1))
+        ctx.enter_context(tc.manual_schedule())
+
+        fock_raw, occ_raw, virt_raw, sb_raw = {}, {}, {}, {}
+        fock_words, fock_banks, fock_q = {}, {}, {}
+        grouped, occ_q, virt_q = {}, {}, {}
+        shifted, r_banks, r_grouped, r_q = {}, {}, {}, {}
+        frac, g_banks, y_f32, y_grouped, y_scales = {}, {}, {}, {}, {}
+
+        def new_bank(group, n):
+            return psum.tile([P, KP], F32, name="bank", tag="%s%d" % (group, n % 4))
+
+        def new_planes(pool, width, tag, bufs):
+            codes = pool.tile([P, width], U32, name="codes", tag=tag + "_codes", bufs=bufs, align_bytes=64)
+            scales = pool.tile([P, width], U8, name="scales", tag=tag + "_scales", bufs=bufs, align_bytes=64)
+            return codes, scales
+
+        def quantize(planes, first, count, source):
+            codes, scales = planes
+            nc.vector.quantize_mx(
+                out=codes[:, first:first + count].bitcast(FP8X4),
+                scales=scales[:, first:first + count],
+                in_=source,
+            )
+
+        def copy_on(engine, out, in_):
+            if engine == "vector":
+                nc.vector.tensor_copy(out=out, in_=in_)
+            else:
+                nc.scalar.copy(out=out, in_=in_)
+
+        def load_fock(h):
+            raw = flow.tile([P, 2 * NB], BF16, name="fock_raw", tag="fock_raw", bufs=4)
+            rows = fock[KP * (h // 2):KP * (h // 2 + 1), :].rearrange("(m t) k -> m t k", t=PACK)
+            nc.sync.dma_start(out=raw[:].rearrange("p (t k) -> p t k", t=2), in_=rows[:, 2 * (h % 2):2 * (h % 2) + 2, :])
+            fock_raw[h] = raw
+
+        def load_rows(store, key, source, tag, bufs):
+            raw = flow.tile([P, PACK, KP], BF16, name="rows_raw", tag=tag, bufs=bufs)
+            nc.sync.dma_start(out=raw[:], in_=source.rearrange("(p j) n -> p j n", j=PACK))
+            store[key] = raw
+
+        def load_occ(g):
+            load_rows(occ_raw, g, c_occ[KP * g:KP * (g + 1), :], "coef_raw", 8)
+
+        def load_virt(u):
+            vb, b = divmod(u, MU_BLOCKS)
+            load_rows(virt_raw, u, c_virt[KP * b:KP * (b + 1), KP * vb:KP * (vb + 1)], "coef_raw", 8)
+
+        def load_sb(b):
+            load_rows(sb_raw, b, shift_block[KP * b:KP * (b + 1), :], "sb_raw", 2)
+
+        def transpose_fock(h):
+            words = fock_raw[h][:].bitcast(F32)
+            for g in range(NU_PASSES):
+                bank = new_bank("turn", NU_PASSES * h + g)
+                for t in range(2):
+                    for u in range(2):
+                        first = t * (NB // 2) + 2 * P * g
+                        nc.tensor.transpose(
+                            bank[:, (2 * t + u) * P:(2 * t + u + 1) * P],
+                            words[:, first + u:first + 2 * P:2],
+                            ident[:],
+                        )
+                fock_banks[h, g] = bank
+
+        def copy_fock(h):
+            stage = flow.tile([P, 2 * NB], BF16, name="fock_words", tag="fock_words", bufs=2, align_bytes=64)
+            for g in range(NU_PASSES):
+                nc.scalar.copy(
+                    out=stage[:].bitcast(F32)[:, KP * g:KP * (g + 1)].rearrange("p (t m u) -> p t m u", t=2, u=2),
+                    in_=fock_banks[h, g][:].rearrange("p (t u m) -> p t m u", t=2, u=2),
+                )
+            fock_words[h] = stage
+
+        def quantize_fock(h):
+            planes = new_planes(flow, NU_PASSES * 2 * P, "fock", 5)
+            quantize(planes, 0, KP, fock_words[h][:, 0:PACK * KP])
+            quantize(planes, KP, 2 * P, fock_words[h][:, PACK * KP:2 * NB])
+            fock_q[h] = planes
+
+        def group_occ(g):
+            tile_g = flow.tile([P, PACK * KP], BF16, name="grouped", tag="grouped", bufs=4, align_bytes=64)
+            nc.vector.tensor_copy(
+                out=tile_g[:].rearrange("p (c i j) -> p c j i", i=4, j=PACK),
+                in_=occ_raw[g][:].rearrange("p j (c i) -> p c j i", i=4),
+            )
+            grouped["occ", g] = tile_g
+
+        def quantize_occ(g):
+            occ_q[g] = new_planes(keep, KP, "occ%d" % g, 1)
+            quantize(occ_q[g], 0, KP, grouped["occ", g][:])
+
+        def group_virt(u, engine):
+            tile_g = flow.tile([P, PACK * KP], BF16, name="grouped", tag="grouped", bufs=4, align_bytes=64)
+            copy_on(
+                engine,
+                tile_g[:].rearrange("p (t a e j) -> p a t e j", t=PACK, e=2, j=PACK),
+                virt_raw[u][:].rearrange("p j (a e t) -> p a t e j", e=2, t=PACK),
+            )
+            grouped["virt", u] = tile_g
+
+        def quantize_virt(u):
+            virt_q[u] = new_planes(keep, KP, "virt%d" % u, 1)
+            quantize(virt_q[u], 0, KP, grouped["virt", u][:])
+
+        def shift_product(b, t):
+            if t == 0:
+                shifted[b] = flow.tile([P, PACK, NO], F32, name="shifted", tag="wide", bufs=3)
+            nc.vector.tensor_tensor(out=shifted[b][:, t, :], in0=sb_raw[b][:, t, :], in1=shift_row[:], op=ALU.mult)
+
+        def half_matmul(b, c):
+            bank = new_bank("acc", PACK * b + c + 2)
+            for t in range(PACK):
+                codes, scales = fock_q[2 * b + t // 2]
+                for g in range(NU_PASSES):
+                    first = 2 * P * g + P * (t % 2)
+                    nc.tensor.matmul_mx(
+                        out=bank[:, P * t:P * (t + 1)],
+                        lhsT=codes[:, first:first + P].bitcast(FP8X4),
+                        lhsT_scale=scales[:, first:first + P],
+                        rhs=occ_q[g][0][:, P * c:P * (c + 1)].bitcast(FP8X4),
+                        rhs_scale=occ_q[g][1][:, P * c:P * (c + 1)],
+                        start=(g == 0),
+                        stop=(g == NU_PASSES - 1),
+                    )
+            r_banks[b, c] = bank
+
+        def add_shift(b, c):
+            if c == 0:
+                r_grouped[b] = flow.tile([P, PACK * NO], BF16, name="r_grouped", tag="r_grouped", bufs=2, align_bytes=64)
+            nc.vector.tensor_tensor(
+                out=r_grouped[b][:, KP * c:KP * (c + 1)].rearrange("p (a e t) -> p a t e", e=2, t=PACK),
+                in0=r_banks[b, c][:].rearrange("p (t a e) -> p a t e", t=PACK, e=2),
+                in1=shifted[b][:, :, P * c:P * (c + 1)].rearrange("p t (a e) -> p a t e", e=2),
+                op=ALU.add,
+            )
+
+        def quantize_r(b):
+            r_q[b] = new_planes(keep, NO, "r%d" % b, 1)
+            quantize(r_q[b], 0, NO, r_grouped[b][:])
+
+        def fraction(vb, t):
+            n = PACK * vb + t
+            frac[vb, t] = keep.tile([P, NO], F32, name="frac", tag="frac%d" % n)
+            nc.scalar.activation(out=frac[vb, t][:], in_=log_occ[:], func=ACT.Sigmoid, scale=-1.0, bias=log_virt[:, n:n + 1])
+
+        def g_pass(vb, t, b, start, stop):
+            if start:
+                g_banks[vb, t] = new_bank("acc" if vb % 2 else "turn", t + (2 if vb % 2 else 0))
+            codes, scales = virt_q[MU_BLOCKS * vb + b]
+            nc.tensor.matmul_mx(
+                out=g_banks[vb, t][:],
+                lhsT=codes[:, P * t:P * (t + 1)].bitcast(FP8X4),
+                lhsT_scale=scales[:, P * t:P * (t + 1)],
+                rhs=r_q[b][0][:].bitcast(FP8X4),
+                rhs_scale=r_q[b][1][:],
+                start=start,
+                stop=stop,
+            )
+
+        def g_matmul(vb, t, blocks):
+            for b in blocks:
+                g_pass(vb, t, b, b == 0, b == MU_BLOCKS - 1)
+
+        def y_rows(vb):
+            return out_0[KP * vb:KP * (vb + 1), :].rearrange("(p t) m -> p t m", t=PACK)
+
+        def divide(vb, t):
+            if t == 0:
+                y_f32[vb] = flow.tile([P, PACK, NO], F32, name="y_f32", tag="wide", bufs=3)
+            n = PACK * vb + t
+            nc.vector.scalar_tensor_tensor(
+                out=y_f32[vb][:, t, :], in0=g_banks[vb, t][:], scalar=neg_inv_virt[:, n:n + 1],
+                in1=frac[vb, t][:], op0=ALU.mult, op1=ALU.mult,
+            )
+            if t % 2:
+                nc.sync.dma_start(out=y_rows(vb)[:, t - 1:t + 1, :], in_=y_f32[vb][:, t - 1:t + 1, :])
+
+        def group_y(vb, engine, first, last):
+            if first == 0:
+                y_grouped[vb] = flow.tile([P, PACK * NO], BF16, name="y_grouped", tag="y_grouped", bufs=3, align_bytes=64)
+            copy_on(
+                engine,
+                y_grouped[vb][:, PACK * first:PACK * last].rearrange("p (a e t) -> p a t e", e=2, t=PACK),
+                y_f32[vb][:, :, first:last].rearrange("p t (a e) -> p a t e", e=2),
+            )
+
+        def quantize_y(vb):
+            codes = keep.tile([P, NO], U32, name="y_codes", tag="y_codes%d" % vb, align_bytes=64)
+            if vb < 2:
+                y_scales[vb] = keep.tile([P, NO], U8, name="y_scales", tag="y_scales%d" % vb, align_bytes=64)
+            nc.vector.quantize_mx(
+                out=codes[:].bitcast(FP8X4), scales=y_scales[min(vb, 1)][4 * (vb // 2):P, :], in_=y_grouped[vb][:]
+            )
+            nc.sync.dma_start(out=out_1[vb].rearrange("p m t -> p (m t)").bitcast(I32), in_=codes[:].bitcast(I32))
+
+        def store_scales(vb, count, second_queue):
+            for q in range(4):
+                queue = second_queue if q % 2 else nc.sync
+                queue.dma_start(
+                    out=out_2[vb:vb + count, 4 * q:4 * q + 4, :].bitcast(I32),
+                    in_=y_scales[vb][32 * q:32 * q + 4 * count, :].bitcast(I32),
+                )
+
+        shift_in = keep.tile([P, PACK], BF16, name="shift_in")
+        occ_in = keep.tile([P, PACK], BF16, name="occ_in")
+        virt_in = keep.tile([P, V_BLOCKS, 16], BF16, name="virt_in")
+        nc.scalar.dma_start(out=occ_in[:], in_=e_occ.rearrange("(p c) -> p c", c=PACK))
+        nc.scalar.dma_start(out=virt_in[:, :, 0:PACK], in_=e_virt.rearrange("(g p t) -> p g t", p=P, t=PACK))
+        nc.scalar.dma_start(out=shift_in[:], in_=shift.rearrange("(p c) -> p c", c=PACK))
+        load_occ(0)
+        load_occ(1)
+        load_fock(0)
+        load_occ(2)
+        load_sb(0)
+        load_fock(1)
+        load_fock(2)
+        load_virt(0)
+        load_sb(1)
+        load_fock(3)
+        load_virt(1)
+
+        ident = keep.tile([P, P], F32, name="ident")
+        make_identity(nc, ident[:])
+
+        log_occ_in = keep.tile([P, PACK], F32, name="log_occ_in")
+        shift_f32 = keep.tile([P, PACK], F32, name="shift_f32")
+        neg_virt = keep.tile([P, V_BLOCKS, PACK], F32, name="neg_virt")
+        neg_inv_virt = keep.tile([P, V_BLOCKS * PACK], F32, name="neg_inv_virt")
+        log_virt = keep.tile([P, V_BLOCKS * PACK], F32, name="log_virt")
+        log_occ = keep.tile([P, NO], F32, name="log_occ")
+        shift_row = keep.tile([P, NO], BF16, name="shift_row")
+        nc.scalar.activation(out=log_occ_in[:], in_=occ_in[:], func=ACT.Ln, scale=-1.0)
+        nc.scalar.activation(
+            out=log_virt[:].rearrange("p (g t) -> p g t", t=PACK), in_=virt_in[:, :, 0:PACK], func=ACT.Ln
+        )
+        nc.vector.tensor_scalar(out=neg_virt[:], in0=virt_in[:, :, 0:PACK], scalar1=-1.0, scalar2=None, op0=ALU.mult)
+        nc.vector.tensor_copy(out=shift_f32[:], in_=shift_in[:])
+        nc.vector.reciprocal(out=neg_inv_virt[:], in_=neg_virt[:].rearrange("p g t -> p (g t)"))
+        spread = []
+        for n, column in enumerate((log_occ_in, shift_f32)):
+            bank = new_bank("acc", n)
+            for c in range(PACK):
+                nc.tensor.transpose(bank[:, P * c:P * (c + 1)], column[:, c:c + 1].to_broadcast([P, P]), ident[:])
+            spread.append(bank[:].rearrange("p (c n) -> p n c", c=PACK))
+        nc.vector.tensor_copy(out=log_occ[:].rearrange("p (n c) -> p n c", c=PACK), in_=spread[0])
+
+        group_occ(0)
+        nc.vector.tensor_copy(out=shift_row[:].rearrange("p (n c) -> p n c", c=PACK), in_=spread[1])
+        quantize_occ(0)
+        group_occ(1)
+        transpose_fock(0)
+        for n in range(0, FRAC_A):
+            fraction(*divmod(n, PACK))
+        copy_fock(0)
+        quantize_occ(1)
+        group_occ(2)
+        shift_product(0, 0)
+        quantize_occ(2)
+        quantize_fock(0)
+        transpose_fock(1)
+        for n in range(FRAC_A, FRAC_B):
+            fraction(*divmod(n, PACK))
+        copy_fock(1)
+        for t in range(1, PACK):
+            shift_product(0, t)
+        quantize_fock(1)
+        transpose_fock(2)
+        for n in range(FRAC_B, V_BLOCKS * PACK):
+            fraction(*divmod(n, PACK))
+
+        ready = []
+        for s in range(HALVES):
+            b, side = divmod(s, 2)
+            if s + 4 < HALVES:
+                load_fock(s + 4)
+            load_virt(s + 2)
+            if side == 0 and b + 2 < MU_BLOCKS:
+                load_sb(b + 2)
+            if s + 2 < HALVES:
+                copy_fock(s + 2)
+            waiting = list(ready)
+            ready.clear()
+            for u in STEP_UNITS[s]:
+                group_virt(u, "scalar")
+                ready.append(u)
+            half_matmul(b, 2 * side)
+            half_matmul(b, 2 * side + 1)
+            if s + 3 < HALVES:
+                transpose_fock(s + 3)
+            if b + 1 < MU_BLOCKS:
+                shift_product(b + 1, 2 * side)
+                shift_product(b + 1, 2 * side + 1)
+            if side == 0 and b > 0:
+                quantize_r(b - 1)
+            for u in waiting:
+                quantize_virt(u)
+            add_shift(b, 2 * side)
+            add_shift(b, 2 * side + 1)
+            if s + 2 < HALVES:
+                quantize_fock(s + 2)
+        load_virt(10)
+        load_virt(11)
+
+        last = MU_BLOCKS - 1
+        group_virt(6, "scalar")
+        quantize_virt(5)
+        for t in range(PACK):
+            g_matmul(0, t, range(last))
+        quantize_r(last)
+        for t in range(PACK):
+            g_matmul(0, t, [last])
+        group_virt(7, "vector")
+        group_virt(8, "scalar")
+        quantize_virt(6)
+        quantize_virt(7)
+        for t in range(PACK):
+            g_matmul(1, t, range(MU_BLOCKS))
+        for t in range(PACK):
+            divide(0, t)
+        group_virt(9, "scalar")
+        group_virt(11, "vector")
+        group_virt(10, "scalar")
+        quantize_virt(8)
+        quantize_virt(11)
+        quantize_virt(9)
+        for b in (0, 3, 1):
+            for t in range(PACK):
+                g_pass(2, t, b, b == 0, False)
+        divide(1, 0)
+        divide(1, 1)
+        quantize_virt(10)
+        for t in range(PACK):
+            g_pass(2, t, 2, False, True)
+        group_y(0, "scalar", 0, NO)
+        divide(1, 2)
+        divide(1, 3)
+        quantize_y(0)
+        store_scales(0, 1, nc.sync)
+        group_y(1, "scalar", 0, NO)
+        for t in range(PACK):
+            divide(2, t)
+        quantize_y(1)
+        group_y(2, "vector", 0, SPLIT)
+        group_y(2, "scalar", SPLIT, NO)
+        quantize_y(2)
+        store_scales(1, 2, nc.scalar)

@@ -23,8 +23,9 @@ MU_BLOCKS = NA // KP
 V_BLOCKS = NV // KP
 HALVES = 2 * MU_BLOCKS
 CV_UNITS = V_BLOCKS * MU_BLOCKS
-FRAC_A, FRAC_B, SPLIT = 5, 9, 288
-STEP_UNITS = [[0], [1], [], [2], [3], [], [4], [5]]
+FRAC_A, SPLIT = 8, 288
+UNIT_ORDER = [(1, 0), (0, 1), (1, 1), (2, 1), (0, 2), (1, 2), (0, 3), (1, 3)]
+STEP_HALVES = [2, 2, 1, 2, 2, 2, 2, 3]
 
 
 def tile_shifted_fock_amplitudes_h3_kernel(
@@ -66,7 +67,7 @@ def tile_shifted_fock_amplitudes_h3_kernel(
                 nc.scalar.copy(out=out, in_=in_)
 
         def load_fock(h):
-            raw = flow.tile([P, 2 * NB], BF16, name="fock_raw", tag="fock_raw", bufs=4)
+            raw = flow.tile([P, 2 * NB], BF16, name="fock_raw", tag="fock_raw", bufs=3)
             rows = fock[KP * (h // 2):KP * (h // 2 + 1), :].rearrange("(m t) k -> m t k", t=PACK)
             nc.sync.dma_start(out=raw[:].rearrange("p (t k) -> p t k", t=2), in_=rows[:, 2 * (h % 2):2 * (h % 2) + 2, :])
             fock_raw[h] = raw
@@ -77,28 +78,34 @@ def tile_shifted_fock_amplitudes_h3_kernel(
             store[key] = raw
 
         def load_occ(g):
-            load_rows(occ_raw, g, c_occ[KP * g:KP * (g + 1), :], "coef_raw", 8)
+            if g == 0:
+                occ_raw["all"] = flow.tile([P, NU_PASSES, PACK, NO], BF16, name="occ_raw", tag="coef_raw", bufs=3)
+            occ_raw[g] = occ_raw["all"][:, g]
+            nc.sync.dma_start(out=occ_raw[g], in_=c_occ[KP * g:KP * (g + 1), :].rearrange("(p j) n -> p j n", j=PACK))
 
-        def load_virt(u):
-            vb, b = divmod(u, MU_BLOCKS)
-            load_rows(virt_raw, u, c_virt[KP * b:KP * (b + 1), KP * vb:KP * (vb + 1)], "coef_raw", 8)
+        def load_virt(b, first=0, last=V_BLOCKS):
+            if first == 0:
+                virt_raw[b] = flow.tile([P, PACK, NV], BF16, name="virt_raw", tag="coef_raw", bufs=3)
+            nc.sync.dma_start(
+                out=virt_raw[b][:, :, KP * first:KP * last],
+                in_=c_virt[KP * b:KP * (b + 1), KP * first:KP * last].rearrange("(p j) n -> p j n", j=PACK),
+            )
 
         def load_sb(b):
             load_rows(sb_raw, b, shift_block[KP * b:KP * (b + 1), :], "sb_raw", 2)
 
-        def transpose_fock(h):
+        def transpose_fock(h, part):
             words = fock_raw[h][:].bitcast(F32)
-            for g in range(NU_PASSES):
-                bank = new_bank("turn", NU_PASSES * h + g)
-                for t in range(2):
-                    for u in range(2):
-                        first = t * (NB // 2) + 2 * P * g
-                        nc.tensor.transpose(
-                            bank[:, (2 * t + u) * P:(2 * t + u + 1) * P],
-                            words[:, first + u:first + 2 * P:2],
-                            ident[:],
-                        )
-                fock_banks[h, g] = bank
+            for n in range(6 * part, 6 * part + 6):
+                g, t, u = n // 4, n // 2 % 2, n % 2
+                if n % 4 == 0:
+                    fock_banks[h, g] = new_bank("turn", NU_PASSES * h + g)
+                first = t * (NB // 2) + 2 * P * g
+                nc.tensor.transpose(
+                    fock_banks[h, g][:, (2 * t + u) * P:(2 * t + u + 1) * P],
+                    words[:, first + u:first + 2 * P:2],
+                    ident[:],
+                )
 
         def copy_fock(h):
             stage = flow.tile([P, 2 * NB], BF16, name="fock_words", tag="fock_words", bufs=2, align_bytes=64)
@@ -110,7 +117,7 @@ def tile_shifted_fock_amplitudes_h3_kernel(
             fock_words[h] = stage
 
         def quantize_fock(h):
-            planes = new_planes(flow, NU_PASSES * 2 * P, "fock", 5)
+            planes = new_planes(flow, NU_PASSES * 2 * P, "fock", 3)
             quantize(planes, 0, KP, fock_words[h][:, 0:PACK * KP])
             quantize(planes, KP, 2 * P, fock_words[h][:, PACK * KP:2 * NB])
             fock_q[h] = planes
@@ -119,7 +126,7 @@ def tile_shifted_fock_amplitudes_h3_kernel(
             tile_g = flow.tile([P, PACK * KP], BF16, name="grouped", tag="grouped", bufs=4, align_bytes=64)
             nc.vector.tensor_copy(
                 out=tile_g[:].rearrange("p (c i j) -> p c j i", i=4, j=PACK),
-                in_=occ_raw[g][:].rearrange("p j (c i) -> p c j i", i=4),
+                in_=occ_raw[g].rearrange("p j (c i) -> p c j i", i=4),
             )
             grouped["occ", g] = tile_g
 
@@ -127,27 +134,29 @@ def tile_shifted_fock_amplitudes_h3_kernel(
             occ_q[g] = new_planes(keep, KP, "occ%d" % g, 1)
             quantize(occ_q[g], 0, KP, grouped["occ", g][:])
 
-        def group_virt(u, engine):
-            tile_g = flow.tile([P, PACK * KP], BF16, name="grouped", tag="grouped", bufs=4, align_bytes=64)
+        def group_virt(vb, b, engine, first=0, last=PACK):
+            if first == 0:
+                grouped["virt", vb, b] = flow.tile([P, PACK * KP], BF16, name="grouped", tag="grouped", bufs=4, align_bytes=64)
             copy_on(
                 engine,
-                tile_g[:].rearrange("p (t a e j) -> p a t e j", t=PACK, e=2, j=PACK),
-                virt_raw[u][:].rearrange("p j (a e t) -> p a t e j", e=2, t=PACK),
+                grouped["virt", vb, b][:].rearrange("p (t a e j) -> p a t e j", t=PACK, e=2, j=PACK)[:, :, first:last],
+                virt_raw[b][:, :, KP * vb:KP * (vb + 1)].rearrange("p j (a e t) -> p a t e j", e=2, t=PACK)[:, :, first:last],
             )
-            grouped["virt", u] = tile_g
 
-        def quantize_virt(u):
-            virt_q[u] = new_planes(keep, KP, "virt%d" % u, 1)
-            quantize(virt_q[u], 0, KP, grouped["virt", u][:])
+        def quantize_virt(vb, b):
+            virt_q[vb, b] = new_planes(keep, KP, "virt%d_%d" % (vb, b), 1)
+            quantize(virt_q[vb, b], 0, KP, grouped["virt", vb, b][:])
 
         def shift_product(b, t):
             if t == 0:
                 shifted[b] = flow.tile([P, PACK, NO], F32, name="shifted", tag="wide", bufs=3)
             nc.vector.tensor_tensor(out=shifted[b][:, t, :], in0=sb_raw[b][:, t, :], in1=shift_row[:], op=ALU.mult)
 
-        def half_matmul(b, c):
-            bank = new_bank("acc", PACK * b + c + 2)
-            for t in range(PACK):
+        def half_matmul(b, c, slots=range(PACK)):
+            if slots[0] == 0:
+                r_banks[b, c] = new_bank("acc", c)
+            bank = r_banks[b, c]
+            for t in slots:
                 codes, scales = fock_q[2 * b + t // 2]
                 for g in range(NU_PASSES):
                     first = 2 * P * g + P * (t % 2)
@@ -160,7 +169,6 @@ def tile_shifted_fock_amplitudes_h3_kernel(
                         start=(g == 0),
                         stop=(g == NU_PASSES - 1),
                     )
-            r_banks[b, c] = bank
 
         def add_shift(b, c):
             if c == 0:
@@ -183,8 +191,8 @@ def tile_shifted_fock_amplitudes_h3_kernel(
 
         def g_pass(vb, t, b, start, stop):
             if start:
-                g_banks[vb, t] = new_bank("acc" if vb % 2 else "turn", t + (2 if vb % 2 else 0))
-            codes, scales = virt_q[MU_BLOCKS * vb + b]
+                g_banks[vb, t] = new_bank("acc" if vb % 2 else "turn", t)
+            codes, scales = virt_q[vb, b]
             nc.tensor.matmul_mx(
                 out=g_banks[vb, t][:],
                 lhsT=codes[:, P * t:P * (t + 1)].bitcast(FP8X4),
@@ -246,16 +254,15 @@ def tile_shifted_fock_amplitudes_h3_kernel(
         nc.scalar.dma_start(out=virt_in[:, :, 0:PACK], in_=e_virt.rearrange("(g p t) -> p g t", p=P, t=PACK))
         nc.scalar.dma_start(out=shift_in[:], in_=shift.rearrange("(p c) -> p c", c=PACK))
         load_occ(0)
-        load_occ(1)
         load_fock(0)
+        load_occ(1)
         load_occ(2)
-        load_sb(0)
         load_fock(1)
+        load_virt(0, 0, 1)
+        load_sb(0)
+        load_virt(0, 1, 2)
         load_fock(2)
-        load_virt(0)
-        load_sb(1)
-        load_fock(3)
-        load_virt(1)
+        load_virt(0, 2, V_BLOCKS)
 
         ident = keep.tile([P, P], F32, name="ident")
         make_identity(nc, ident[:])
@@ -265,118 +272,141 @@ def tile_shifted_fock_amplitudes_h3_kernel(
         neg_virt = keep.tile([P, V_BLOCKS, PACK], F32, name="neg_virt")
         neg_inv_virt = keep.tile([P, V_BLOCKS * PACK], F32, name="neg_inv_virt")
         log_virt = keep.tile([P, V_BLOCKS * PACK], F32, name="log_virt")
-        log_occ = keep.tile([P, NO], F32, name="log_occ")
         shift_row = keep.tile([P, NO], BF16, name="shift_row")
         nc.scalar.activation(out=log_occ_in[:], in_=occ_in[:], func=ACT.Ln, scale=-1.0)
         nc.scalar.activation(
             out=log_virt[:].rearrange("p (g t) -> p g t", t=PACK), in_=virt_in[:, :, 0:PACK], func=ACT.Ln
         )
-        nc.vector.tensor_scalar(out=neg_virt[:], in0=virt_in[:, :, 0:PACK], scalar1=-1.0, scalar2=None, op0=ALU.mult)
-        nc.vector.tensor_copy(out=shift_f32[:], in_=shift_in[:])
-        nc.vector.reciprocal(out=neg_inv_virt[:], in_=neg_virt[:].rearrange("p g t -> p (g t)"))
-        spread = []
-        for n, column in enumerate((log_occ_in, shift_f32)):
-            bank = new_bank("acc", n)
-            for c in range(PACK):
-                nc.tensor.transpose(bank[:, P * c:P * (c + 1)], column[:, c:c + 1].to_broadcast([P, P]), ident[:])
-            spread.append(bank[:].rearrange("p (c n) -> p n c", c=PACK))
-        nc.vector.tensor_copy(out=log_occ[:].rearrange("p (n c) -> p n c", c=PACK), in_=spread[0])
+        log_occ = new_bank("acc", 3)
 
+        def spread(bank, column):
+            for c in range(PACK):
+                nc.tensor.transpose(bank[:, c:NO:PACK], column[:, c:c + 1].to_broadcast([P, P]), ident[:])
+
+        spread(log_occ, log_occ_in)
         group_occ(0)
-        nc.vector.tensor_copy(out=shift_row[:].rearrange("p (n c) -> p n c", c=PACK), in_=spread[1])
+        nc.vector.tensor_scalar(out=neg_virt[:], in0=virt_in[:, :, 0:PACK], scalar1=-1.0, scalar2=None, op0=ALU.mult)
         quantize_occ(0)
+        nc.vector.tensor_copy(out=shift_f32[:], in_=shift_in[:])
+        transpose_fock(0, 0)
+        transpose_fock(0, 1)
+        shift_bank = new_bank("acc", 2)
+        spread(shift_bank, shift_f32)
         group_occ(1)
-        transpose_fock(0)
+        nc.vector.reciprocal(out=neg_inv_virt[:], in_=neg_virt[:].rearrange("p g t -> p (g t)"))
+        group_occ(2)
+        quantize_occ(1)
+        quantize_occ(2)
+        nc.vector.tensor_copy(out=shift_row[:], in_=shift_bank[:])
         for n in range(0, FRAC_A):
             fraction(*divmod(n, PACK))
         copy_fock(0)
-        quantize_occ(1)
-        group_occ(2)
-        shift_product(0, 0)
-        quantize_occ(2)
+        load_fock(3)
+        load_virt(1, 0, 1)
+        transpose_fock(1, 0)
+        transpose_fock(1, 1)
         quantize_fock(0)
-        transpose_fock(1)
-        for n in range(FRAC_A, FRAC_B):
-            fraction(*divmod(n, PACK))
-        copy_fock(1)
-        for t in range(1, PACK):
-            shift_product(0, t)
-        quantize_fock(1)
-        transpose_fock(2)
-        for n in range(FRAC_B, V_BLOCKS * PACK):
+        group_virt(0, 0, "vector")
+        for n in range(FRAC_A, V_BLOCKS * PACK):
             fraction(*divmod(n, PACK))
 
-        ready = []
-        for s in range(HALVES):
-            b, side = divmod(s, 2)
-            if s + 4 < HALVES:
-                load_fock(s + 4)
-            load_virt(s + 2)
-            if side == 0 and b + 2 < MU_BLOCKS:
-                load_sb(b + 2)
-            if s + 2 < HALVES:
-                copy_fock(s + 2)
-            waiting = list(ready)
-            ready.clear()
-            for u in STEP_UNITS[s]:
-                group_virt(u, "scalar")
-                ready.append(u)
-            half_matmul(b, 2 * side)
-            half_matmul(b, 2 * side + 1)
-            if s + 3 < HALVES:
-                transpose_fock(s + 3)
-            if b + 1 < MU_BLOCKS:
-                shift_product(b + 1, 2 * side)
-                shift_product(b + 1, 2 * side + 1)
+        halves = [(vb, b, first) for vb, b in UNIT_ORDER for first in (0, 2)]
+        done = 0
+        quantized = 0
+        for h in range(HALVES):
+            b, side = divmod(h, 2)
+            if h + 4 < HALVES:
+                load_fock(h + 4)
+            if side == 0 and b + 1 < MU_BLOCKS:
+                load_sb(b + 1)
+            if h == 0:
+                load_virt(1, 1, V_BLOCKS)
+            if side == 0 and 0 < b < MU_BLOCKS - 1:
+                load_virt(b + 1)
+            waiting = UNIT_ORDER[quantized:done // 2]
+            quantized = done // 2
+            if h + 1 < HALVES:
+                copy_fock(h + 1)
+            for vb, vm, first in halves[done:done + STEP_HALVES[h]]:
+                group_virt(vb, vm, "scalar", first, first + 2)
+            done = done + STEP_HALVES[h]
             if side == 0 and b > 0:
-                quantize_r(b - 1)
-            for u in waiting:
-                quantize_virt(u)
-            add_shift(b, 2 * side)
-            add_shift(b, 2 * side + 1)
-            if s + 2 < HALVES:
-                quantize_fock(s + 2)
-        load_virt(10)
-        load_virt(11)
+                add_shift(b - 1, 2)
+                add_shift(b - 1, 3)
+            for pair in range(2):
+                half_matmul(b, 2 * pair, range(2 * side, 2 * side + 2))
+                half_matmul(b, 2 * pair + 1, range(2 * side, 2 * side + 2))
+                if h + 2 < HALVES:
+                    transpose_fock(h + 2, pair)
+                elif side == 1:
+                    for t in range(PACK):
+                        g_matmul(0, t, [pair])
+            if side == 0:
+                shift_product(b, 0)
+                shift_product(b, 1)
+                quantize_fock(h + 1)
+                if b > 0:
+                    quantize_r(b - 1)
+                else:
+                    quantize_virt(0, 0)
+                shift_product(b, 2)
+                shift_product(b, 3)
+            else:
+                for u in waiting[:1]:
+                    quantize_virt(*u)
+                if b == 0:
+                    group_virt(2, 0, "vector")
+                add_shift(b, 0)
+                add_shift(b, 1)
+                if h + 1 < HALVES:
+                    quantize_fock(h + 1)
+                for u in waiting[1:]:
+                    quantize_virt(*u)
+                if b == 0:
+                    quantize_virt(2, 0)
+            if side == 0:
+                quantized = quantized - len(waiting)
 
         last = MU_BLOCKS - 1
-        group_virt(6, "scalar")
-        quantize_virt(5)
+        add_shift(last, 2)
+        add_shift(last, 3)
         for t in range(PACK):
-            g_matmul(0, t, range(last))
+            g_matmul(0, t, [2])
+        quantize_virt(0, 3)
         quantize_r(last)
+        group_virt(2, 2, "scalar")
+        group_virt(2, 3, "scalar")
+        for t in range(2):
+            g_matmul(1, t, range(3))
         for t in range(PACK):
             g_matmul(0, t, [last])
-        group_virt(7, "vector")
-        group_virt(8, "scalar")
-        quantize_virt(6)
-        quantize_virt(7)
-        for t in range(PACK):
+        quantize_virt(1, 3)
+        for t in range(2):
+            g_matmul(1, t, [last])
+        for t in range(2, PACK):
             g_matmul(1, t, range(MU_BLOCKS))
         for t in range(PACK):
             divide(0, t)
-        group_virt(9, "scalar")
-        group_virt(11, "vector")
-        group_virt(10, "scalar")
-        quantize_virt(8)
-        quantize_virt(11)
-        quantize_virt(9)
-        for b in (0, 3, 1):
-            for t in range(PACK):
-                g_pass(2, t, b, b == 0, False)
+        quantize_virt(2, 2)
+        for t in range(2):
+            g_matmul(2, t, range(last))
+        group_y(0, "scalar", 0, NO)
         divide(1, 0)
         divide(1, 1)
-        quantize_virt(10)
-        for t in range(PACK):
-            g_pass(2, t, 2, False, True)
-        group_y(0, "scalar", 0, NO)
+        quantize_virt(2, 3)
+        for t in range(2):
+            g_matmul(2, t, [last])
+        for t in range(2, PACK):
+            g_matmul(2, t, range(MU_BLOCKS))
         divide(1, 2)
         divide(1, 3)
+        group_y(1, "scalar", 0, NO)
+        divide(2, 0)
+        divide(2, 1)
         quantize_y(0)
         store_scales(0, 1, nc.sync)
-        group_y(1, "scalar", 0, NO)
-        for t in range(PACK):
-            divide(2, t)
+        divide(2, 2)
+        divide(2, 3)
         quantize_y(1)
         group_y(2, "vector", 0, SPLIT)
         group_y(2, "scalar", SPLIT, NO)

@@ -23,9 +23,7 @@ MU_BLOCKS = NA // KP
 V_BLOCKS = NV // KP
 HALVES = 2 * MU_BLOCKS
 CV_UNITS = V_BLOCKS * MU_BLOCKS
-FRAC_A, SPLIT = 8, 288
-UNIT_ORDER = [(1, 0), (0, 1), (1, 1), (2, 1), (0, 2), (1, 2), (0, 3), (1, 3)]
-STEP_HALVES = [2, 2, 1, 2, 2, 2, 2, 3]
+FRAC_A, FRAC_B, SPLIT = 6, 9, 304
 
 
 def tile_shifted_fock_amplitudes_h3_kernel(
@@ -78,55 +76,49 @@ def tile_shifted_fock_amplitudes_h3_kernel(
             store[key] = raw
 
         def load_occ(g):
-            if g == 0:
-                occ_raw["all"] = flow.tile([P, NU_PASSES, PACK, NO], BF16, name="occ_raw", tag="coef_raw", bufs=3)
-            occ_raw[g] = occ_raw["all"][:, g]
-            nc.sync.dma_start(out=occ_raw[g], in_=c_occ[KP * g:KP * (g + 1), :].rearrange("(p j) n -> p j n", j=PACK))
+            load_rows(occ_raw, g, c_occ[KP * g:KP * (g + 1), :], "coef_raw", 8)
 
-        def load_virt(b, first=0, last=V_BLOCKS):
-            if first == 0:
-                virt_raw[b] = flow.tile([P, PACK, NV], BF16, name="virt_raw", tag="coef_raw", bufs=3)
-            nc.sync.dma_start(
-                out=virt_raw[b][:, :, KP * first:KP * last],
-                in_=c_virt[KP * b:KP * (b + 1), KP * first:KP * last].rearrange("(p j) n -> p j n", j=PACK),
-            )
+        def load_virt(vb, b):
+            load_rows(virt_raw, (vb, b), c_virt[KP * b:KP * (b + 1), KP * vb:KP * (vb + 1)], "coef_raw", 8)
 
         def load_sb(b):
             load_rows(sb_raw, b, shift_block[KP * b:KP * (b + 1), :], "sb_raw", 2)
 
-        def transpose_fock(h, part):
-            words = fock_raw[h][:].bitcast(F32)
-            for n in range(6 * part, 6 * part + 6):
-                g, t, u = n // 4, n // 2 % 2, n % 2
-                if n % 4 == 0:
-                    fock_banks[h, g] = new_bank("turn", NU_PASSES * h + g)
-                first = t * (NB // 2) + 2 * P * g
-                nc.tensor.transpose(
-                    fock_banks[h, g][:, (2 * t + u) * P:(2 * t + u + 1) * P],
-                    words[:, first + u:first + 2 * P:2],
-                    ident[:],
-                )
+        def transpose_fock(first, last):
+            for n in range(first, last):
+                h, g = divmod(n, NU_PASSES)
+                words = fock_raw[h][:].bitcast(F32)
+                fock_banks[n] = new_bank("turn", n)
+                for t in range(2):
+                    start = t * (NB // 2) + 2 * P * g
+                    for u in range(2):
+                        nc.tensor.transpose(
+                            fock_banks[n][:, (2 * t + u) * P:(2 * t + u + 1) * P],
+                            words[:, start + u:start + 2 * P:2],
+                            ident[:],
+                        )
 
-        def copy_fock(h):
-            stage = flow.tile([P, 2 * NB], BF16, name="fock_words", tag="fock_words", bufs=2, align_bytes=64)
-            for g in range(NU_PASSES):
+        def copy_fock(first, last):
+            for n in range(first, last):
+                h, g = divmod(n, NU_PASSES)
+                if g == 0:
+                    fock_words[h] = flow.tile([P, 2 * NB], BF16, name="fock_words", tag="fock_words", bufs=2, align_bytes=64)
                 nc.scalar.copy(
-                    out=stage[:].bitcast(F32)[:, KP * g:KP * (g + 1)].rearrange("p (t m u) -> p t m u", t=2, u=2),
-                    in_=fock_banks[h, g][:].rearrange("p (t u m) -> p t m u", t=2, u=2),
+                    out=fock_words[h][:].bitcast(F32)[:, KP * g:KP * (g + 1)].rearrange("p (t m u) -> p t m u", t=2, u=2),
+                    in_=fock_banks[n][:].rearrange("p (t u m) -> p t m u", t=2, u=2),
                 )
-            fock_words[h] = stage
 
         def quantize_fock(h):
-            planes = new_planes(flow, NU_PASSES * 2 * P, "fock", 3)
+            planes = new_planes(flow, NU_PASSES * 2 * P, "fock", 5)
             quantize(planes, 0, KP, fock_words[h][:, 0:PACK * KP])
             quantize(planes, KP, 2 * P, fock_words[h][:, PACK * KP:2 * NB])
             fock_q[h] = planes
 
         def group_occ(g):
-            tile_g = flow.tile([P, PACK * KP], BF16, name="grouped", tag="grouped", bufs=4, align_bytes=64)
+            tile_g = flow.tile([P, PACK * KP], BF16, name="grouped", tag="grouped", bufs=5, align_bytes=64)
             nc.vector.tensor_copy(
                 out=tile_g[:].rearrange("p (c i j) -> p c j i", i=4, j=PACK),
-                in_=occ_raw[g].rearrange("p j (c i) -> p c j i", i=4),
+                in_=occ_raw[g][:].rearrange("p j (c i) -> p c j i", i=4),
             )
             grouped["occ", g] = tile_g
 
@@ -136,11 +128,11 @@ def tile_shifted_fock_amplitudes_h3_kernel(
 
         def group_virt(vb, b, engine, first=0, last=PACK):
             if first == 0:
-                grouped["virt", vb, b] = flow.tile([P, PACK * KP], BF16, name="grouped", tag="grouped", bufs=4, align_bytes=64)
+                grouped["virt", vb, b] = flow.tile([P, PACK * KP], BF16, name="grouped", tag="grouped", bufs=5, align_bytes=64)
             copy_on(
                 engine,
                 grouped["virt", vb, b][:].rearrange("p (t a e j) -> p a t e j", t=PACK, e=2, j=PACK)[:, :, first:last],
-                virt_raw[b][:, :, KP * vb:KP * (vb + 1)].rearrange("p j (a e t) -> p a t e j", e=2, t=PACK)[:, :, first:last],
+                virt_raw[vb, b][:].rearrange("p j (a e t) -> p a t e j", e=2, t=PACK)[:, :, first:last],
             )
 
         def quantize_virt(vb, b):
@@ -258,11 +250,8 @@ def tile_shifted_fock_amplitudes_h3_kernel(
         load_occ(1)
         load_occ(2)
         load_fock(1)
-        load_virt(0, 0, 1)
-        load_sb(0)
-        load_virt(0, 1, 2)
         load_fock(2)
-        load_virt(0, 2, V_BLOCKS)
+        load_sb(0)
 
         ident = keep.tile([P, P], F32, name="ident")
         make_identity(nc, ident[:])
@@ -288,8 +277,7 @@ def tile_shifted_fock_amplitudes_h3_kernel(
         nc.vector.tensor_scalar(out=neg_virt[:], in0=virt_in[:, :, 0:PACK], scalar1=-1.0, scalar2=None, op0=ALU.mult)
         quantize_occ(0)
         nc.vector.tensor_copy(out=shift_f32[:], in_=shift_in[:])
-        transpose_fock(0, 0)
-        transpose_fock(0, 1)
+        transpose_fock(0, 3)
         shift_bank = new_bank("acc", 2)
         spread(shift_bank, shift_f32)
         group_occ(1)
@@ -300,113 +288,154 @@ def tile_shifted_fock_amplitudes_h3_kernel(
         nc.vector.tensor_copy(out=shift_row[:], in_=shift_bank[:])
         for n in range(0, FRAC_A):
             fraction(*divmod(n, PACK))
-        copy_fock(0)
+        copy_fock(0, 3)
+        load_virt(0, 1)
+        load_virt(0, 0)
         load_fock(3)
-        load_virt(1, 0, 1)
-        transpose_fock(1, 0)
-        transpose_fock(1, 1)
+        transpose_fock(3, 7)
         quantize_fock(0)
-        group_virt(0, 0, "vector")
-        for n in range(FRAC_A, V_BLOCKS * PACK):
+        for n in range(FRAC_A, FRAC_B):
             fraction(*divmod(n, PACK))
+        copy_fock(3, 6)
+        transpose_fock(7, 8)
+        load_fock(4)
+        load_sb(1)
+        shift_product(0, 0)
+        shift_product(0, 1)
+        quantize_fock(1)
+        shift_product(0, 2)
+        shift_product(0, 3)
+        for n in range(FRAC_B, V_BLOCKS * PACK):
+            fraction(*divmod(n, PACK))
+        copy_fock(6, 8)
 
-        halves = [(vb, b, first) for vb, b in UNIT_ORDER for first in (0, 2)]
-        done = 0
-        quantized = 0
-        for h in range(HALVES):
-            b, side = divmod(h, 2)
-            if h + 4 < HALVES:
-                load_fock(h + 4)
-            if side == 0 and b + 1 < MU_BLOCKS:
-                load_sb(b + 1)
-            if h == 0:
-                load_virt(1, 1, V_BLOCKS)
-            if side == 0 and 0 < b < MU_BLOCKS - 1:
-                load_virt(b + 1)
-            waiting = UNIT_ORDER[quantized:done // 2]
-            quantized = done // 2
-            if h + 1 < HALVES:
-                copy_fock(h + 1)
-            for vb, vm, first in halves[done:done + STEP_HALVES[h]]:
-                group_virt(vb, vm, "scalar", first, first + 2)
-            done = done + STEP_HALVES[h]
-            if side == 0 and b > 0:
-                add_shift(b - 1, 2)
-                add_shift(b - 1, 3)
-            for pair in range(2):
-                half_matmul(b, 2 * pair, range(2 * side, 2 * side + 2))
-                half_matmul(b, 2 * pair + 1, range(2 * side, 2 * side + 2))
-                if h + 2 < HALVES:
-                    transpose_fock(h + 2, pair)
-                elif side == 1:
-                    for t in range(PACK):
-                        g_matmul(0, t, [pair])
-            if side == 0:
-                shift_product(b, 0)
-                shift_product(b, 1)
-                quantize_fock(h + 1)
-                if b > 0:
-                    quantize_r(b - 1)
-                else:
-                    quantize_virt(0, 0)
-                shift_product(b, 2)
-                shift_product(b, 3)
-            else:
-                for u in waiting[:1]:
-                    quantize_virt(*u)
-                if b == 0:
-                    group_virt(2, 0, "vector")
-                add_shift(b, 0)
-                add_shift(b, 1)
-                if h + 1 < HALVES:
-                    quantize_fock(h + 1)
-                for u in waiting[1:]:
-                    quantize_virt(*u)
-                if b == 0:
-                    quantize_virt(2, 0)
-            if side == 0:
-                quantized = quantized - len(waiting)
-
-        last = MU_BLOCKS - 1
-        add_shift(last, 2)
-        add_shift(last, 3)
+        half_matmul(0, 0)
+        half_matmul(0, 1)
+        transpose_fock(8, 12)
+        load_virt(0, 2)
+        load_fock(5)
+        load_virt(0, 3)
+        load_fock(6)
+        group_virt(0, 0, "vector")
+        add_shift(0, 0)
+        add_shift(0, 1)
+        group_virt(0, 1, "scalar")
+        copy_fock(8, 12)
+        quantize_virt(0, 0)
+        quantize_fock(2)
+        half_matmul(0, 2)
+        half_matmul(0, 3)
+        transpose_fock(12, 16)
+        load_sb(2)
+        load_fock(7)
+        load_virt(1, 0)
+        shift_product(1, 0)
+        quantize_fock(3)
+        add_shift(0, 2)
+        add_shift(0, 3)
+        group_virt(0, 2, "scalar", 0, 2)
+        copy_fock(12, 16)
+        shift_product(1, 1)
+        quantize_r(0)
+        shift_product(1, 2)
+        shift_product(1, 3)
+        load_sb(3)
+        load_virt(1, 1)
+        load_virt(1, 2)
+        load_virt(1, 3)
+        half_matmul(1, 0)
+        half_matmul(1, 1)
+        transpose_fock(16, 20)
+        quantize_virt(0, 1)
+        quantize_fock(4)
+        add_shift(1, 0)
+        add_shift(1, 1)
+        group_virt(0, 2, "scalar", 2, 4)
+        group_virt(0, 3, "scalar", 0, 2)
+        copy_fock(16, 20)
+        shift_product(2, 0)
+        shift_product(2, 1)
+        shift_product(2, 2)
+        quantize_virt(0, 2)
+        half_matmul(1, 2)
+        half_matmul(1, 3)
+        transpose_fock(20, 24)
+        load_virt(2, 0)
+        load_virt(2, 1)
+        quantize_fock(5)
+        add_shift(1, 2)
+        add_shift(1, 3)
+        group_virt(0, 3, "scalar", 2, 4)
+        group_virt(1, 0, "scalar", 0, 2)
+        copy_fock(20, 24)
+        shift_product(2, 3)
+        quantize_r(1)
+        load_virt(2, 2)
+        load_virt(2, 3)
+        for c in range(PACK):
+            half_matmul(2, c)
+        group_virt(1, 0, "scalar", 2, 4)
+        shift_product(3, 0)
+        quantize_virt(0, 3)
+        group_virt(1, 1, "vector")
+        add_shift(2, 0)
+        add_shift(2, 1)
+        quantize_fock(6)
+        add_shift(2, 2)
+        add_shift(2, 3)
+        quantize_fock(7)
+        for t in range(PACK):
+            g_matmul(0, t, range(2))
+        group_virt(1, 2, "scalar")
+        quantize_r(2)
+        shift_product(3, 1)
+        shift_product(3, 2)
+        shift_product(3, 3)
+        for c in range(PACK):
+            half_matmul(3, c)
         for t in range(PACK):
             g_matmul(0, t, [2])
-        quantize_virt(0, 3)
-        quantize_r(last)
+        group_virt(1, 3, "scalar")
+        quantize_virt(1, 0)
+        add_shift(3, 0)
+        add_shift(3, 1)
+        quantize_virt(1, 1)
+        group_virt(2, 0, "scalar")
+        add_shift(3, 2)
+        add_shift(3, 3)
+        for t in range(PACK):
+            g_matmul(1, t, range(2))
+        quantize_virt(1, 2)
+        quantize_r(3)
+        group_virt(2, 1, "scalar")
+        for t in range(PACK):
+            g_matmul(0, t, [3])
+        quantize_virt(1, 3)
+        for t in range(PACK):
+            g_matmul(1, t, range(2, 4))
+        quantize_virt(2, 0)
         group_virt(2, 2, "scalar")
         group_virt(2, 3, "scalar")
-        for t in range(2):
-            g_matmul(1, t, range(3))
-        for t in range(PACK):
-            g_matmul(0, t, [last])
-        quantize_virt(1, 3)
-        for t in range(2):
-            g_matmul(1, t, [last])
-        for t in range(2, PACK):
-            g_matmul(1, t, range(MU_BLOCKS))
         for t in range(PACK):
             divide(0, t)
-        quantize_virt(2, 2)
-        for t in range(2):
-            g_matmul(2, t, range(last))
+        quantize_virt(2, 1)
+        for b in range(2):
+            for t in range(PACK):
+                g_matmul(2, t, [b])
         group_y(0, "scalar", 0, NO)
         divide(1, 0)
         divide(1, 1)
+        quantize_virt(2, 2)
         quantize_virt(2, 3)
-        for t in range(2):
-            g_matmul(2, t, [last])
-        for t in range(2, PACK):
-            g_matmul(2, t, range(MU_BLOCKS))
+        for t in range(PACK):
+            g_matmul(2, t, range(2, MU_BLOCKS))
         divide(1, 2)
         divide(1, 3)
         group_y(1, "scalar", 0, NO)
-        divide(2, 0)
-        divide(2, 1)
         quantize_y(0)
         store_scales(0, 1, nc.sync)
-        divide(2, 2)
-        divide(2, 3)
+        for t in range(PACK):
+            divide(2, t)
         quantize_y(1)
         group_y(2, "vector", 0, SPLIT)
         group_y(2, "scalar", SPLIT, NO)

from contextlib import ExitStack

import concourse.mybir as mybir
from concourse.masks import make_identity

NA, NB, NO, NV = 2048, 1536, 512, 1536
FLOPS = 2 * NA * NB * NO + 2 * NA * NV * NO

F32 = mybir.dt.float32
BF16 = mybir.dt.bfloat16
I32 = mybir.dt.int32
U32 = mybir.dt.uint32
U8 = mybir.dt.uint8
FP8X4 = mybir.dt.float8_e4m3fn_x4
ACT = mybir.ActivationFunctionType
ALU = mybir.AluOpType

P = 128
PACK = 4
KP = P * PACK
NU_PASSES = NB // KP
MU_BLOCKS = NA // KP
V_BLOCKS = NV // KP
HALVES = 2 * MU_BLOCKS
CV_UNITS = V_BLOCKS * MU_BLOCKS
FRAC_A, FRAC_B, SPLIT = 6, 9, 304


def tile_shifted_fock_amplitudes_h3_kernel(
    tc, fock, c_occ, shift_block, shift, c_virt, e_occ, e_virt, out_0, out_1, out_2
):
    nc = tc.nc
    with ExitStack() as ctx:
        keep = ctx.enter_context(tc.tile_pool(name="keep", bufs=1))
        flow = ctx.enter_context(tc.tile_pool(name="flow", bufs=2))
        psum = ctx.enter_context(tc.psum_pool(name="psum", bufs=1))
        ctx.enter_context(tc.manual_schedule())

        fock_raw, occ_raw, virt_raw, sb_raw = {}, {}, {}, {}
        fock_words, fock_banks, fock_q = {}, {}, {}
        grouped, occ_q, virt_q = {}, {}, {}
        shifted, r_banks, r_grouped, r_q = {}, {}, {}, {}
        frac, g_banks, y_f32, y_grouped, y_scales = {}, {}, {}, {}, {}

        def new_bank(group, n):
            return psum.tile([P, KP], F32, name="bank", tag="%s%d" % (group, n % 4))

        def new_planes(pool, width, tag, bufs):
            codes = pool.tile([P, width], U32, name="codes", tag=tag + "_codes", bufs=bufs, align_bytes=64)
            scales = pool.tile([P, width], U8, name="scales", tag=tag + "_scales", bufs=bufs, align_bytes=64)
            return codes, scales

        def quantize(planes, first, count, source):
            codes, scales = planes
            nc.vector.quantize_mx(
                out=codes[:, first:first + count].bitcast(FP8X4),
                scales=scales[:, first:first + count],
                in_=source,
            )

        def copy_on(engine, out, in_):
            if engine == "vector":
                nc.vector.tensor_copy(out=out, in_=in_)
            else:
                nc.scalar.copy(out=out, in_=in_)

        def load_fock(h):
            raw = flow.tile([P, 2 * NB], BF16, name="fock_raw", tag="fock_raw", bufs=3)
            rows = fock[KP * (h // 2):KP * (h // 2 + 1), :].rearrange("(m t) k -> m t k", t=PACK)
            nc.sync.dma_start(out=raw[:].rearrange("p (t k) -> p t k", t=2), in_=rows[:, 2 * (h % 2):2 * (h % 2) + 2, :])
            fock_raw[h] = raw

        def load_rows(store, key, source, tag, bufs):
            raw = flow.tile([P, PACK, KP], BF16, name="rows_raw", tag=tag, bufs=bufs)
            nc.sync.dma_start(out=raw[:], in_=source.rearrange("(p j) n -> p j n", j=PACK))
            store[key] = raw

        def load_occ(g):
            load_rows(occ_raw, g, c_occ[KP * g:KP * (g + 1), :], "coef_raw", 8)

        def load_virt(vb, b):
            load_rows(virt_raw, (vb, b), c_virt[KP * b:KP * (b + 1), KP * vb:KP * (vb + 1)], "coef_raw", 8)

        def load_sb(b):
            load_rows(sb_raw, b, shift_block[KP * b:KP * (b + 1), :], "sb_raw", 2)

        def transpose_fock(first, last):
            for n in range(first, last):
                h, g = divmod(n, NU_PASSES)
                words = fock_raw[h][:].bitcast(F32)
                fock_banks[n] = new_bank("turn", n)
                for t in range(2):
                    start = t * (NB // 2) + 2 * P * g
                    for u in range(2):
                        nc.tensor.transpose(
                            fock_banks[n][:, (2 * t + u) * P:(2 * t + u + 1) * P],
                            words[:, start + u:start + 2 * P:2],
                            ident[:],
                        )

        def copy_fock(first, last):
            for n in range(first, last):
                h, g = divmod(n, NU_PASSES)
                if g == 0:
                    fock_words[h] = flow.tile([P, 2 * NB], BF16, name="fock_words", tag="fock_words", bufs=2, align_bytes=64)
                nc.scalar.copy(
                    out=fock_words[h][:].bitcast(F32)[:, KP * g:KP * (g + 1)].rearrange("p (t m u) -> p t m u", t=2, u=2),
                    in_=fock_banks[n][:].rearrange("p (t u m) -> p t m u", t=2, u=2),
                )

        def quantize_fock(h):
            planes = new_planes(flow, NU_PASSES * 2 * P, "fock", 5)
            quantize(planes, 0, KP, fock_words[h][:, 0:PACK * KP])
            quantize(planes, KP, 2 * P, fock_words[h][:, PACK * KP:2 * NB])
            fock_q[h] = planes

        def group_occ(g):
            tile_g = flow.tile([P, PACK * KP], BF16, name="grouped", tag="grouped", bufs=5, align_bytes=64)
            nc.vector.tensor_copy(
                out=tile_g[:].rearrange("p (c i j) -> p c j i", i=4, j=PACK),
                in_=occ_raw[g][:].rearrange("p j (c i) -> p c j i", i=4),
            )
            grouped["occ", g] = tile_g

        def quantize_occ(g):
            occ_q[g] = new_planes(keep, KP, "occ%d" % g, 1)
            quantize(occ_q[g], 0, KP, grouped["occ", g][:])

        def group_virt(vb, b, engine, first=0, last=PACK):
            if first == 0:
                grouped["virt", vb, b] = flow.tile([P, PACK * KP], BF16, name="grouped", tag="grouped", bufs=5, align_bytes=64)
            copy_on(
                engine,
                grouped["virt", vb, b][:].rearrange("p (t a e j) -> p a t e j", t=PACK, e=2, j=PACK)[:, :, first:last],
                virt_raw[vb, b][:].rearrange("p j (a e t) -> p a t e j", e=2, t=PACK)[:, :, first:last],
            )

        def quantize_virt(vb, b):
            virt_q[vb, b] = new_planes(keep, KP, "virt%d_%d" % (vb, b), 1)
            quantize(virt_q[vb, b], 0, KP, grouped["virt", vb, b][:])

        def shift_product(b, t):
            if t == 0:
                shifted[b] = flow.tile([P, PACK, NO], F32, name="shifted", tag="wide", bufs=3)
            nc.vector.tensor_tensor(out=shifted[b][:, t, :], in0=sb_raw[b][:, t, :], in1=shift_row[:], op=ALU.mult)

        def half_matmul(b, c, slots=range(PACK)):
            if slots[0] == 0:
                r_banks[b, c] = new_bank("acc", c)
            bank = r_banks[b, c]
            for t in slots:
                codes, scales = fock_q[2 * b + t // 2]
                for g in range(NU_PASSES):
                    first = 2 * P * g + P * (t % 2)
                    nc.tensor.matmul_mx(
                        out=bank[:, P * t:P * (t + 1)],
                        lhsT=codes[:, first:first + P].bitcast(FP8X4),
                        lhsT_scale=scales[:, first:first + P],
                        rhs=occ_q[g][0][:, P * c:P * (c + 1)].bitcast(FP8X4),
                        rhs_scale=occ_q[g][1][:, P * c:P * (c + 1)],
                        start=(g == 0),
                        stop=(g == NU_PASSES - 1),
                    )

        def add_shift(b, c):
            if c == 0:
                r_grouped[b] = flow.tile([P, PACK * NO], BF16, name="r_grouped", tag="r_grouped", bufs=2, align_bytes=64)
            nc.vector.tensor_tensor(
                out=r_grouped[b][:, KP * c:KP * (c + 1)].rearrange("p (a e t) -> p a t e", e=2, t=PACK),
                in0=r_banks[b, c][:].rearrange("p (t a e) -> p a t e", t=PACK, e=2),
                in1=shifted[b][:, :, P * c:P * (c + 1)].rearrange("p t (a e) -> p a t e", e=2),
                op=ALU.add,
            )

        def quantize_r(b):
            r_q[b] = new_planes(keep, NO, "r%d" % b, 1)
            quantize(r_q[b], 0, NO, r_grouped[b][:])

        def fraction(vb, t):
            n = PACK * vb + t
            frac[vb, t] = keep.tile([P, NO], F32, name="frac", tag="frac%d" % n)
            nc.scalar.activation(out=frac[vb, t][:], in_=log_occ[:], func=ACT.Sigmoid, scale=-1.0, bias=log_virt[:, n:n + 1])

        def g_pass(vb, t, b, start, stop):
            if start:
                g_banks[vb, t] = new_bank("acc" if vb % 2 else "turn", t)
            codes, scales = virt_q[vb, b]
            nc.tensor.matmul_mx(
                out=g_banks[vb, t][:],
                lhsT=codes[:, P * t:P * (t + 1)].bitcast(FP8X4),
                lhsT_scale=scales[:, P * t:P * (t + 1)],
                rhs=r_q[b][0][:].bitcast(FP8X4),
                rhs_scale=r_q[b][1][:],
                start=start,
                stop=stop,
            )

        def g_matmul(vb, t, blocks):
            for b in blocks:
                g_pass(vb, t, b, b == 0, b == MU_BLOCKS - 1)

        def y_rows(vb):
            return out_0[KP * vb:KP * (vb + 1), :].rearrange("(p t) m -> p t m", t=PACK)

        def divide(vb, t):
            if t == 0:
                y_f32[vb] = flow.tile([P, PACK, NO], F32, name="y_f32", tag="wide", bufs=3)
            n = PACK * vb + t
            nc.vector.scalar_tensor_tensor(
                out=y_f32[vb][:, t, :], in0=g_banks[vb, t][:], scalar=neg_inv_virt[:, n:n + 1],
                in1=frac[vb, t][:], op0=ALU.mult, op1=ALU.mult,
            )
            if t % 2:
                nc.sync.dma_start(out=y_rows(vb)[:, t - 1:t + 1, :], in_=y_f32[vb][:, t - 1:t + 1, :])

        def group_y(vb, engine, first, last):
            if first == 0:
                y_grouped[vb] = flow.tile([P, PACK * NO], BF16, name="y_grouped", tag="y_grouped", bufs=3, align_bytes=64)
            copy_on(
                engine,
                y_grouped[vb][:, PACK * first:PACK * last].rearrange("p (a e t) -> p a t e", e=2, t=PACK),
                y_f32[vb][:, :, first:last].rearrange("p t (a e) -> p a t e", e=2),
            )

        def quantize_y(vb):
            codes = keep.tile([P, NO], U32, name="y_codes", tag="y_codes%d" % vb, align_bytes=64)
            if vb < 2:
                y_scales[vb] = keep.tile([P, NO], U8, name="y_scales", tag="y_scales%d" % vb, align_bytes=64)
            nc.vector.quantize_mx(
                out=codes[:].bitcast(FP8X4), scales=y_scales[min(vb, 1)][4 * (vb // 2):P, :], in_=y_grouped[vb][:]
            )
            nc.sync.dma_start(out=out_1[vb].rearrange("p m t -> p (m t)").bitcast(I32), in_=codes[:].bitcast(I32))

        def store_scales(vb, count, second_queue):
            for q in range(4):
                queue = second_queue if q % 2 else nc.sync
                queue.dma_start(
                    out=out_2[vb:vb + count, 4 * q:4 * q + 4, :].bitcast(I32),
                    in_=y_scales[vb][32 * q:32 * q + 4 * count, :].bitcast(I32),
                )

        shift_in = keep.tile([P, PACK], BF16, name="shift_in")
        occ_in = keep.tile([P, PACK], BF16, name="occ_in")
        virt_in = keep.tile([P, V_BLOCKS, 16], BF16, name="virt_in")
        nc.scalar.dma_start(out=occ_in[:], in_=e_occ.rearrange("(p c) -> p c", c=PACK))
        nc.scalar.dma_start(out=virt_in[:, :, 0:PACK], in_=e_virt.rearrange("(g p t) -> p g t", p=P, t=PACK))
        nc.scalar.dma_start(out=shift_in[:], in_=shift.rearrange("(p c) -> p c", c=PACK))
        load_occ(0)
        load_fock(0)
        load_occ(1)
        load_occ(2)
        load_fock(1)
        load_fock(2)
        load_sb(0)

        ident = keep.tile([P, P], F32, name="ident")
        make_identity(nc, ident[:])

        log_occ_in = keep.tile([P, PACK], F32, name="log_occ_in")
        shift_f32 = keep.tile([P, PACK], F32, name="shift_f32")
        neg_virt = keep.tile([P, V_BLOCKS, PACK], F32, name="neg_virt")
        neg_inv_virt = keep.tile([P, V_BLOCKS * PACK], F32, name="neg_inv_virt")
        log_virt = keep.tile([P, V_BLOCKS * PACK], F32, name="log_virt")
        shift_row = keep.tile([P, NO], BF16, name="shift_row")
        nc.scalar.activation(out=log_occ_in[:], in_=occ_in[:], func=ACT.Ln, scale=-1.0)
        nc.scalar.activation(
            out=log_virt[:].rearrange("p (g t) -> p g t", t=PACK), in_=virt_in[:, :, 0:PACK], func=ACT.Ln
        )
        log_occ = new_bank("acc", 3)

        def spread(bank, column):
            for c in range(PACK):
                nc.tensor.transpose(bank[:, c:NO:PACK], column[:, c:c + 1].to_broadcast([P, P]), ident[:])

        spread(log_occ, log_occ_in)
        group_occ(0)
        nc.vector.tensor_scalar(out=neg_virt[:], in0=virt_in[:, :, 0:PACK], scalar1=-1.0, scalar2=None, op0=ALU.mult)
        quantize_occ(0)
        nc.vector.tensor_copy(out=shift_f32[:], in_=shift_in[:])
        transpose_fock(0, 3)
        shift_bank = new_bank("acc", 2)
        spread(shift_bank, shift_f32)
        group_occ(1)
        nc.vector.reciprocal(out=neg_inv_virt[:], in_=neg_virt[:].rearrange("p g t -> p (g t)"))
        group_occ(2)
        quantize_occ(1)
        quantize_occ(2)
        nc.vector.tensor_copy(out=shift_row[:], in_=shift_bank[:])
        for n in range(0, FRAC_A):
            fraction(*divmod(n, PACK))
        copy_fock(0, 3)
        load_virt(0, 1)
        load_virt(0, 0)
        load_fock(3)
        transpose_fock(3, 7)
        quantize_fock(0)
        for n in range(FRAC_A, FRAC_B):
            fraction(*divmod(n, PACK))
        copy_fock(3, 6)
        transpose_fock(7, 8)
        load_fock(4)
        load_sb(1)
        shift_product(0, 0)
        shift_product(0, 1)
        quantize_fock(1)
        shift_product(0, 2)
        shift_product(0, 3)
        for n in range(FRAC_B, V_BLOCKS * PACK):
            fraction(*divmod(n, PACK))
        copy_fock(6, 8)

        half_matmul(0, 0)
        half_matmul(0, 1)
        transpose_fock(8, 12)
        load_virt(0, 2)
        load_fock(5)
        load_virt(0, 3)
        load_fock(6)
        group_virt(0, 0, "vector")
        add_shift(0, 0)
        add_shift(0, 1)
        group_virt(0, 1, "scalar")
        copy_fock(8, 12)
        quantize_virt(0, 0)
        quantize_fock(2)
        half_matmul(0, 2)
        half_matmul(0, 3)
        transpose_fock(12, 16)
        load_sb(2)
        load_fock(7)
        load_virt(1, 0)
        shift_product(1, 0)
        quantize_fock(3)
        add_shift(0, 2)
        add_shift(0, 3)
        group_virt(0, 2, "scalar", 0, 2)
        copy_fock(12, 16)
        shift_product(1, 1)
        quantize_r(0)
        shift_product(1, 2)
        shift_product(1, 3)
        load_sb(3)
        load_virt(1, 1)
        load_virt(1, 2)
        load_virt(1, 3)
        half_matmul(1, 0)
        half_matmul(1, 1)
        transpose_fock(16, 20)
        quantize_virt(0, 1)
        quantize_fock(4)
        add_shift(1, 0)
        add_shift(1, 1)
        group_virt(0, 2, "scalar", 2, 4)
        group_virt(0, 3, "scalar", 0, 2)
        copy_fock(16, 20)
        shift_product(2, 0)
        shift_product(2, 1)
        shift_product(2, 2)
        quantize_virt(0, 2)
        half_matmul(1, 2)
        half_matmul(1, 3)
        transpose_fock(20, 24)
        load_virt(2, 0)
        load_virt(2, 1)
        quantize_fock(5)
        add_shift(1, 2)
        add_shift(1, 3)
        group_virt(0, 3, "scalar", 2, 4)
        group_virt(1, 0, "scalar", 0, 2)
        copy_fock(20, 24)
        shift_product(2, 3)
        quantize_r(1)
        load_virt(2, 2)
        load_virt(2, 3)
        for c in range(PACK):
            half_matmul(2, c)
        group_virt(1, 0, "scalar", 2, 4)
        shift_product(3, 0)
        quantize_virt(0, 3)
        group_virt(1, 1, "vector")
        add_shift(2, 0)
        add_shift(2, 1)
        quantize_fock(6)
        add_shift(2, 2)
        add_shift(2, 3)
        quantize_fock(7)
        for t in range(PACK):
            g_matmul(0, t, range(2))
        group_virt(1, 2, "scalar")
        quantize_r(2)
        shift_product(3, 1)
        shift_product(3, 2)
        shift_product(3, 3)
        for c in range(PACK):
            half_matmul(3, c)
        for t in range(PACK):
            g_matmul(0, t, [2])
        group_virt(1, 3, "scalar")
        quantize_virt(1, 0)
        add_shift(3, 0)
        add_shift(3, 1)
        quantize_virt(1, 1)
        group_virt(2, 0, "scalar")
        add_shift(3, 2)
        add_shift(3, 3)
        for t in range(PACK):
            g_matmul(1, t, range(2))
        quantize_virt(1, 2)
        quantize_r(3)
        group_virt(2, 1, "scalar")
        for t in range(PACK):
            g_matmul(0, t, [3])
        quantize_virt(1, 3)
        for t in range(PACK):
            g_matmul(1, t, range(2, 4))
        quantize_virt(2, 0)
        group_virt(2, 2, "scalar")
        group_virt(2, 3, "scalar")
        for t in range(PACK):
            divide(0, t)
        quantize_virt(2, 1)
        for b in range(2):
            for t in range(PACK):
                g_matmul(2, t, [b])
        group_y(0, "scalar", 0, NO)
        divide(1, 0)
        divide(1, 1)
        quantize_virt(2, 2)
        quantize_virt(2, 3)
        for t in range(PACK):
            g_matmul(2, t, range(2, MU_BLOCKS))
        divide(1, 2)
        divide(1, 3)
        group_y(1, "scalar", 0, NO)
        quantize_y(0)
        store_scales(0, 1, nc.sync)
        for t in range(PACK):
            divide(2, t)
        quantize_y(1)
        group_y(2, "vector", 0, SPLIT)
        group_y(2, "scalar", SPLIT, NO)
        quantize_y(2)
        store_scales(1, 2, nc.scalar)
